import numpy as np
import ml_dtypes


def mxq(x, axis, fmt="e4m3"):
    dtype, down = {"e4m3": (ml_dtypes.float8_e4m3fn, 7), "e5m2": (ml_dtypes.float8_e5m2, 14)}[fmt]
    v = np.moveaxis(np.asarray(x, np.float32).astype(ml_dtypes.bfloat16).astype(np.float64), axis, -1)
    blocks = v.reshape(v.shape[:-1] + (-1, 32))
    amax = np.abs(blocks).max(-1, keepdims=True)
    byte = np.maximum(np.where(amax > 0, np.frexp(amax)[1] - 1 + 127, 0) - down, 1)
    scale = np.exp2(byte - 127.0)
    codes = (blocks / scale).astype(np.float32).astype(dtype).astype(np.float64)
    return np.moveaxis((codes * scale).reshape(v.shape), -1, axis)


WIDE = False


def mx_kscale(k):
    if not WIDE:
        return np.ones(k)
    levels = np.array([10, -10, 5, -5, 0])
    if k % 512:
        return np.exp2(np.random.permutation(np.resize(levels, k // 32))).repeat(32)
    a = np.empty((k // 512, 16))
    for p in range(k // 512):
        a[p, :8] = np.random.permutation(np.resize(levels, 8))
        for g in range(8):
            far = levels[np.abs(levels - a[p, g]) >= 10]
            a[p, g + 8] = far[np.random.randint(len(far))]
    return np.exp2(a.ravel()).repeat(32)


def f64(x):
    return np.asarray(x).astype(np.float64)


def striped(idx):
    return np.tile(idx.reshape(-1, 16).T, (8, 1)).astype(np.uint16)


def unstriped(offs):
    return offs[:16].T.reshape(-1).astype(np.int64)


def gelu(v):
    return 0.5 * v * (1.0 + np.tanh(np.sqrt(2.0 / np.pi) * (v + 0.044715 * v**3)))


K, T, E, C, H, N = 512, 512, 4, 256, 512, 512


def by_expert(wq, xq):
    return np.concatenate([wq[e].T @ xq[:, e * C:(e + 1) * C] for e in range(E)], axis=1)


def setup_inputs():
    n = np.random.standard_normal
    s = mx_kscale(K)[:, None]
    u = mx_kscale(H)
    first = np.random.permutation(np.repeat(np.arange(E), T // E))
    second = (first + 1 + np.random.permutation(np.repeat(np.arange(E - 1), -(-T // (E - 1)))[:T])) % E
    while np.bincount(second, minlength=E).max() != T // E:
        load = np.bincount(second, minlength=E); hi, lo = int(load.argmax()), int(load.argmin())
        t = np.flatnonzero((second == hi) & (first != lo))[0]; second[t] = lo
    slot_token = np.empty(E * C, np.int64); pos = np.empty((2, T), np.int64); fill = np.zeros(E, np.int64)
    place = np.stack([np.random.permutation(C) for _ in range(E)])
    for r, deal in enumerate((first, second)):
        for t in np.random.permutation(T):
            e = deal[t]; j = e * C + place[e, fill[e]]; fill[e] += 1; slot_token[j] = t; pos[r, t] = j
    g = np.random.uniform(0.2, 0.8, T)
    return {
        "xT": (n((K, T)) * s).astype(np.float32),
        "w1": (n((E + 1, K, H)) / np.sqrt(K) / s[None] * u[None, None, :]).astype(np.float32),
        "w2": (n((E + 1, H, N)) / np.sqrt(H) / u[None, :, None]).astype(np.float32),
        "gate": np.stack([np.tile(g, (N, 1)), np.tile(1.0 - g, (N, 1))]).astype(np.float32),
        "offs": striped(slot_token),
        "pos1": striped(pos[0]),
        "pos2": striped(pos[1]),
    }


def reference(xT, w1, w2, gate, offs, pos1, pos2):
    idx = unstriped(offs)
    w1q, w2q = mxq(f64(w1), 1, "e4m3"), mxq(f64(w2), 1, "e4m3")
    xs = mxq(f64(xT), 0, "e4m3")
    hs = gelu(w1q[E].T @ xs)
    ys = w2q[E].T @ mxq(hs, 0, "e4m3")
    xq = mxq(f64(xT)[:, idx], 0, "e4m3")
    h = gelu(by_expert(w1q, xq))
    y = by_expert(w2q, mxq(h, 0, "e4m3"))
    return ys + f64(gate[0]) * y[:, unstriped(pos1)] + f64(gate[1]) * y[:, unstriped(pos2)]

@@ -1,0 +1,303 @@
+from contextlib import ExitStack
+
+import concourse.mybir as mybir
+
+F32 = mybir.dt.float32
+BF16 = mybir.dt.bfloat16
+U32 = mybir.dt.uint32
+U16 = mybir.dt.uint16
+U8 = mybir.dt.uint8
+FP8X4 = mybir.dt.float8_e4m3fn_x4
+MULT = mybir.AluOpType.mult
+ADD = mybir.AluOpType.add
+GELU = mybir.ActivationFunctionType.Gelu_apprx_tanh
+
+K, T, E, C, H, N = 512, 512, 4, 256, 512, 512
+P = 128
+FLOPS = 2 * (E * C + T) * (K * H + H * N)
+BYTES = 4 * (K * T + (E + 1) * (K * H + H * N) + 2 * T + N * T) + 2 * P * (E * C + 2 * T) // 16
+
+DMA = ['x0', 'w10', 'x1', 'w11', 'w12', 'w13', 'w20.0', 'w21.0', 'w22.0', 'w23.0', 'gate', 'w20.1', 'w21.1', 'w22.1', 'w23.1', 'w14', 'w24.0', 'w24.1']
+ORDER = """
+X 0 S 0 512;
+G 0 0;
+W1 0 S 64 128;
+W1 0 V 0 64;
+G 1 0;
+X 1 S 0 512;
+G 2 0;
+Q1 0;
+G 3 0;
+W1 1 S 64 128;
+G 0 1;
+G 1 1;
+QX 0;
+QX 1;
+W1 1 V 0 64;
+M 0 0;
+W1 2 S 64 128;
+M 0 1;
+G 2 1;
+A 0 0;
+Q1 1;
+A 0 1;
+QX 2;
+W1 2 V 0 64;
+M 1 0;
+W1 3 S 64 128;
+M 1 1;
+QH 0;
+Q1 2;
+A 1 0;
+G 3 1;
+A 1 1;
+M 2 0;
+W1 3 V 0 64;
+W2 0 0 S 96 256;
+M 2 1;
+QH 1;
+A 2 0;
+QX 3;
+Q1 3;
+A 2 1;
+W2 0 0 V 0 96;
+W2 1 0 S 96 256;
+W2 1 0 V 0 96;
+M 3 0;
+QH 2;
+W2 2 0 S 96 256;
+M 3 1;
+Q2 0 0;
+Q2 1 0;
+A 3 0;
+W2 2 0 V 0 96;
+W2 3 0 V 0 96;
+N 0 0;
+A 3 1;
+Q2 2 0;
+N 0 1;
+XS;
+W2 3 0 S 96 256;
+QH 3;
+Y 0 0;
+W2 0 1 V 0 64;
+Q2 3 0;
+Y 0 1;
+W2 1 1 V 0 64;
+XQ;
+W2 0 1 S 64 256;
+N 1 0;
+N 1 1;
+W2 2 1 V 0 64;
+Y 1 0;
+Q2 0 1;
+Y 1 1;
+GA 0;
+W2 1 1 S 64 256;
+W2 2 1 S 64 256;
+W2 3 1 V 0 64;
+GB 0;
+W2 3 1 S 64 256;
+Q2 1 1;
+W1 4 S 0 64;
+Q2 2 1;
+AD 0;
+N 0 2;
+N 0 3;
+Q2 3 1;
+Y 0 2;
+GA 1;
+N 1 2;
+Y 0 3;
+N 1 3;
+W1 4 S 64 128;
+GB 1;
+Y 1 2;
+AD 1;
+Y 1 3;
+Q1 4;
+W2 4 0 S 0 256;
+GA 2;
+M 4 0;
+W2 4 1 S 0 256;
+M 4 1;
+GB 2;
+M 4 2;
+M 4 3;
+A 4 0;
+Q2 4 0;
+A 4 1;
+Q2 4 1;
+AD 2;
+A 4 2;
+GA 3;
+A 4 3;
+QH 4;
+GB 3;
+S 0;
+S 1;
+S 2;
+F 0;
+S 3;
+AD 3;
+F 1;
+F 2;
+F 3
+"""
+
+
+def tile_moe_shr_mlp_gelu_kernel(tc, xT, w1, w2, gate, offs, pos1, pos2, out):
+    nc = tc.nc
+    with ExitStack() as ctx:
+        lists = ctx.enter_context(tc.tile_pool(name="lists", bufs=1))
+        keep = ctx.enter_context(tc.tile_pool(name="keep", bufs=1))
+        group = ctx.enter_context(tc.tile_pool(name="group", bufs=4))
+        group2 = ctx.enter_context(tc.tile_pool(name="group2", bufs=4))
+        ring = ctx.enter_context(tc.tile_pool(name="ring", bufs=4))
+        psum_a = ctx.enter_context(tc.psum_pool(name="psum_a", bufs=2))
+        psum_y = ctx.enter_context(tc.psum_pool(name="psum_y", bufs=2))
+        psum_s = ctx.enter_context(tc.psum_pool(name="psum_s", bufs=1))
+
+        offs_t = lists.tile([P, E * C // 16], U16, name="offs_t")
+        pos_t = [lists.tile([P, T // 16], U16, name=f"pos_t{r}") for r in range(2)]
+        x_raw = keep.tile([P, 4, T], F32, name="x_raw")
+        w1_raw = [keep.tile([P, 4, H], F32, name=f"w1_raw{e}") for e in range(E + 1)]
+        w2_raw = [[keep.tile([P, 4, N // 2], F32, name=f"w2_raw{e}_{h}") for h in range(2)] for e in range(E + 1)]
+        gates = keep.tile([P, 2, T], F32, name="gates")
+
+        xr = xT.rearrange("(p j) t -> p j t", j=4)
+        nc.sync.dma_start(offs_t[:], offs)
+        for d in DMA:
+            if d.startswith("x"):
+                u = int(d[1])
+                nc.sync.dma_start(out=x_raw[:, 2 * u:2 * u + 2, :], in_=xr[:, 2 * u:2 * u + 2, :])
+            elif d == "gate":
+                nc.sync.dma_start(pos_t[0][:], pos1)
+                nc.sync.dma_start(pos_t[1][:], pos2)
+                nc.sync.dma_start(out=gates[:], in_=gate[:, 0:P, :].rearrange("g p t -> p g t"))
+            elif d.startswith("w1"):
+                e = int(d[2])
+                nc.sync.dma_start(out=w1_raw[e][:], in_=w1[e].rearrange("(p j) i -> p j i", j=4))
+            else:
+                e, h = int(d[2]), int(d[4])
+                nc.sync.dma_start(out=w2_raw[e][h][:], in_=w2[e].rearrange("(p j) n -> p j n", j=4)[:, :, h * 256:(h + 1) * 256])
+
+        warm = keep.tile([P, 1], F32, name="warm")
+        nc.vector.memset(warm[:], 0.0)
+        nc.scalar.activation(warm[:], warm[:], GELU)
+
+        def copy_on(engine, dst, src):
+            if engine == "V":
+                nc.vector.tensor_copy(out=dst, in_=src)
+            elif engine == "S":
+                nc.scalar.copy(out=dst, in_=src)
+            else:
+                nc.gpsimd.tensor_scalar(out=dst, in0=src, scalar1=1.0, scalar2=0.0, op0=MULT, op1=ADD)
+
+        def quantize(grouped, width, name):
+            codes = keep.tile([P, width], U32, name=name + "_c", align_bytes=64)
+            scales = keep.tile([P, width], U8, name=name + "_s", align_bytes=64)
+            nc.vector.quantize_mx(out=codes[:].bitcast(FP8X4), scales=scales[:], in_=grouped)
+            return codes, scales
+
+        def mx(dst, a, acols, b, bcols):
+            nc.tensor.matmul_mx(
+                out=dst, lhsT=a[0][:, acols].bitcast(FP8X4), lhsT_scale=a[1][:, acols],
+                rhs=b[0][:, bcols].bitcast(FP8X4), rhs_scale=b[1][:, bcols], start=True, stop=True)
+
+        xw = keep.tile([P, 2, T, 2], BF16, name="xw", align_bytes=64)
+        words = xw[:].rearrange("p u t e -> p (u t e)").bitcast(U32)
+        y = [keep.tile([P, E * C], F32, name=f"y{m}") for m in range(4)]
+        xs = keep.tile([P, T, 2, 2], BF16, name="xs", align_bytes=64)
+        st = {}
+
+        def get(key, make):
+            if key not in st:
+                st[key] = make()
+            return st[key]
+
+        for step in ORDER.replace("\n", "").split(";"):
+            f = step.split()
+            k = f[0]
+            n = [int(z) for z in f[1:] if z not in ("V", "S", "G")]
+            eng = [z for z in f[1:] if z in ("V", "S", "G")]
+            if k == "X":
+                u, a, b = n
+                copy_on(eng[0], xw[:, u, a:b], x_raw[:, 2 * u:2 * u + 2, a:b].rearrange("p e t -> p t e"))
+            elif k == "G":
+                e, u = n
+                xg = get(f"xg{e}", lambda: ring.tile([P, 4 * C], BF16, name="xg", align_bytes=64))
+                xgw = xg[:].bitcast(U32).rearrange("p (n u) -> p n u", u=2)
+                nc.vector.tensor_copy(
+                    out=xgw[:, :, u], in_=words[:, u * T:(u + 1) * T].indirect(offs_t[:, e * C // 16:(e + 1) * C // 16]))
+            elif k == "QX":
+                st[f"xq{n[0]}"] = quantize(st[f"xg{n[0]}"][:], C, f"xq{n[0]}")
+            elif k == "XS":
+                nc.vector.tensor_copy(out=xs[:], in_=xw[:].rearrange("p u t e -> p t u e"))
+            elif k == "XQ":
+                st["xq4"] = quantize(xs[:].rearrange("p t u e -> p (t u e)"), T, "xsq")
+            elif k == "W1":
+                e, a, b = n
+                g = get(f"g1{e}", lambda: group.tile([P, 4 * H], BF16, name="wg1", align_bytes=64))
+                copy_on(eng[0], g[:].rearrange("p (t m j) -> p m j t", t=4, j=4)[:, a:b],
+                        w1_raw[e][:].rearrange("p j (m t) -> p m j t", t=4)[:, a:b])
+            elif k == "Q1":
+                st[f"w1q{n[0]}"] = quantize(st[f"g1{n[0]}"][:], H, f"w1q{n[0]}")
+            elif k == "W2":
+                e, h, a, b = n
+                g = get(f"g2{e}_{h}", lambda: group2.tile([P, 2 * N], BF16, name="wg2", align_bytes=64))
+                copy_on(eng[0], g[:].rearrange("p (c i j) -> p c j i", i=4, j=4)[:, a // 4:b // 4],
+                        w2_raw[e][h][:].rearrange("p j (c i) -> p c j i", i=4)[:, a // 4:b // 4])
+            elif k == "Q2":
+                e, h = n
+                st[f"w2q{e}_{h}"] = quantize(st[f"g2{e}_{h}"][:], N // 2, f"w2q{e}_{h}")
+            elif k == "M":
+                e, c = n
+                bank = psum_a.tile([P, 4, P], F32, name="bank_a")
+                st[f"ba{e}_{c}"] = bank
+                for r in range(4):
+                    mx(bank[:, r, :], st[f"w1q{e}"], slice(P * r, P * r + P), st[f"xq{e}"], slice(P * c, P * c + P))
+            elif k == "A":
+                e, c = n
+                if e < E:
+                    hg = get(f"hg{e}", lambda: ring.tile([P, C, 4], BF16, name="hg", align_bytes=64))
+                else:
+                    hg = get(f"hg{e}", lambda: keep.tile([P, T, 4], BF16, name="hs", align_bytes=64))
+                nc.scalar.activation(hg[:, P * c:P * c + P, :], st[f"ba{e}_{c}"][:].rearrange("p r n -> p n r"), GELU)
+            elif k == "QH":
+                e = n[0]
+                st[f"hq{e}"] = quantize(st[f"hg{e}"][:].rearrange("p n r -> p (n r)"), C if e < E else T, f"hq{e}")
+            elif k == "N":
+                pr, m = n
+                bank = psum_y.tile([P, 2, C], F32, name="bank_y")
+                st[f"by{pr}_{m}"] = bank
+                for i in range(2):
+                    mx(bank[:, i, :], st[f"w2q{2 * pr + i}_{m // 2}"], slice(P * (m % 2), P * (m % 2) + P), st[f"hq{2 * pr + i}"], slice(0, C))
+            elif k == "Y":
+                pr, m = n
+                copy_on("S", y[m][:, 512 * pr:512 * pr + 512], st[f"by{pr}_{m}"][:].rearrange("p i n -> p (i n)"))
+            elif k == "S":
+                m = n[0]
+                bank = psum_s.tile([P, T], F32, name=f"bank_s{m}")
+                mx(bank[:], st[f"w2q4_{m // 2}"], slice(P * (m % 2), P * (m % 2) + P), st["hq4"], slice(0, T))
+                st[f"ys{m}"] = bank
+            elif k == "GA":
+                m = n[0]
+                first = ring.tile([P, T], F32, name="first")
+                st[f"ga{m}"] = first
+                nc.vector.tensor_tensor(first[:], y[m][:].indirect(pos_t[0][:]), gates[:, 0, :], MULT)
+            elif k == "GB":
+                m = n[0]
+                second = ring.tile([P, T], F32, name="second")
+                st[f"gb{m}"] = second
+                nc.vector.tensor_tensor(second[:], y[m][:].indirect(pos_t[1][:]), gates[:, 1, :], MULT)
+            elif k == "AD":
+                m = n[0]
+                both = keep.tile([P, T], F32, name=f"both{m}")
+                st[f"ad{m}"] = both
+                nc.vector.tensor_tensor(both[:], st[f"ga{m}"][:], st[f"gb{m}"][:], ADD)
+            elif k == "F":
+                m = n[0]
+                res = ring.tile([P, T], F32, name="res")
+                nc.vector.tensor_tensor(res[:], st[f"ys{m}"][:], st[f"ad{m}"][:], ADD)
+                nc.sync.dma_start(out=out[P * m:P * m + P, :], in_=res[:])

@@ -17,121 +17,127 @@ P = 128
 FLOPS = 2 * (E * C + T) * (K * H + H * N)
 BYTES = 4 * (K * T + (E + 1) * (K * H + H * N) + 2 * T + N * T) + 2 * P * (E * C + 2 * T) // 16
 
-DMA = ['x0', 'w10', 'x1', 'w11', 'w12', 'w13', 'w20.0', 'w21.0', 'w22.0', 'w23.0', 'gate', 'w20.1', 'w21.1', 'w22.1', 'w23.1', 'w14', 'w24.0', 'w24.1']
+DMA = ["x0","x1","w10","w11","w12","w13","w20.0","w21.0","w22.0","w23.0","gate","w20.1","w21.1","w22.1","w23.1","w14","w24.0","w24.1"]
 ORDER = """
-X 0 S 0 512;
+X 0 V 0 448;
+X 0 S 448 512;
 G 0 0;
-W1 0 S 64 128;
-W1 0 V 0 64;
+X 1 S 192 512;
+X 1 V 0 192;
 G 1 0;
-X 1 S 0 512;
+XS 0 S 256 512;
 G 2 0;
-Q1 0;
 G 3 0;
-W1 1 S 64 128;
+W1 0 S 48 128;
 G 0 1;
 G 1 1;
-QX 0;
-QX 1;
-W1 1 V 0 64;
-M 0 0;
-W1 2 S 64 128;
-M 0 1;
 G 2 1;
-A 0 0;
-Q1 1;
-A 0 1;
-QX 2;
-W1 2 V 0 64;
-M 1 0;
-W1 3 S 64 128;
-M 1 1;
-QH 0;
-Q1 2;
-A 1 0;
+I 0;
 G 3 1;
+I 1;
+W1 0 V 0 48;
+QX 0;
+W1 1 S 48 128;
+Q1 0;
+QX 1;
+W1 1 V 0 48;
+M 0 0;
+I 2;
+M 0 1;
+W1 2 V 0 128;
+A 0 0;
+A 0 1;
+Q1 1;
+I 3;
+QX 2;
+QH 0;
+M 1 0;
+W1 3 S 96 128;
+Q1 2;
+M 1 1;
+A 1 0;
+QX 3;
+W1 3 V 0 96;
 A 1 1;
 M 2 0;
-W1 3 V 0 64;
-W2 0 0 S 96 256;
+W2 0.0 S 128 256;
+W2 0.0 V 0 128;
 M 2 1;
 QH 1;
 A 2 0;
-QX 3;
 Q1 3;
 A 2 1;
-W2 0 0 V 0 96;
-W2 1 0 S 96 256;
-W2 1 0 V 0 96;
+Q2 0.0;
+W2 1.0 V 0 96;
+W2 1.0 S 96 256;
 M 3 0;
-QH 2;
-W2 2 0 S 96 256;
+W2 2.0 V 0 256;
 M 3 1;
-Q2 0 0;
-Q2 1 0;
 A 3 0;
-W2 2 0 V 0 96;
-W2 3 0 V 0 96;
-N 0 0;
+Q2 1.0;
 A 3 1;
-Q2 2 0;
+Q2 2.0;
+W2 3.0 V 0 224;
+QH 2;
+N 0 0;
+W2 3.0 S 224 256;
 N 0 1;
-XS;
-W2 3 0 S 96 256;
 QH 3;
 Y 0 0;
-W2 0 1 V 0 64;
-Q2 3 0;
+Q2 3.0;
+XS 0 V 0 256;
 Y 0 1;
-W2 1 1 V 0 64;
-XQ;
-W2 0 1 S 64 256;
 N 1 0;
+W2 0.1 V 0 96;
+W2 0.1 S 96 256;
+XQ;
 N 1 1;
-W2 2 1 V 0 64;
 Y 1 0;
-Q2 0 1;
+Q2 0.1;
 Y 1 1;
+W2 1.1 V 0 192;
+W2 1.1 S 192 256;
 GA 0;
-W2 1 1 S 64 256;
-W2 2 1 S 64 256;
-W2 3 1 V 0 64;
+W2 2.1 S 0 256;
+Q2 1.1;
 GB 0;
-W2 3 1 S 64 256;
-Q2 1 1;
-W1 4 S 0 64;
-Q2 2 1;
-AD 0;
 N 0 2;
+W2 3.1 S 0 256;
 N 0 3;
-Q2 3 1;
+Q2 2.1;
+AD 0;
 Y 0 2;
 GA 1;
-N 1 2;
 Y 0 3;
-N 1 3;
-W1 4 S 64 128;
+W1 4 S 16 72;
+Q2 3.1;
+W1 4 V 0 16;
 GB 1;
-Y 1 2;
+N 1 2;
+N 1 3;
+W1 4 S 72 128;
+W2 4.0 V 0 32;
 AD 1;
-Y 1 3;
+Y 1 2;
+W2 4.1 V 0 160;
 Q1 4;
-W2 4 0 S 0 256;
+Y 1 3;
 GA 2;
+W2 4.0 S 32 256;
 M 4 0;
-W2 4 1 S 0 256;
 M 4 1;
 GB 2;
-M 4 2;
-M 4 3;
 A 4 0;
-Q2 4 0;
 A 4 1;
-Q2 4 1;
+M 4 2;
+Q2 4.0;
+W2 4.1 S 160 256;
 AD 2;
+M 4 3;
 A 4 2;
 GA 3;
 A 4 3;
+Q2 4.1;
 QH 4;
 GB 3;
 S 0;
@@ -219,21 +225,27 @@ def tile_moe_shr_mlp_gelu_kernel(tc, xT, w1, w2, gate, offs, pos1, pos2, out):
         for step in ORDER.replace("\n", "").split(";"):
             f = step.split()
             k = f[0]
-            n = [int(z) for z in f[1:] if z not in ("V", "S", "G")]
+            n = [int(z) for part in f[1:] if part not in ("V", "S", "G") for z in part.split(".")]
             eng = [z for z in f[1:] if z in ("V", "S", "G")]
             if k == "X":
                 u, a, b = n
                 copy_on(eng[0], xw[:, u, a:b], x_raw[:, 2 * u:2 * u + 2, a:b].rearrange("p e t -> p t e"))
             elif k == "G":
                 e, u = n
-                xg = get(f"xg{e}", lambda: ring.tile([P, 4 * C], BF16, name="xg", align_bytes=64))
-                xgw = xg[:].bitcast(U32).rearrange("p (n u) -> p n u", u=2)
+                gw = get(f"gw{e}", lambda: keep.tile([P, 2, C, 2], BF16, name=f"gw{e}", align_bytes=64))
+                gww = gw[:].rearrange("p u n e -> p (u n e)").bitcast(U32)
                 nc.vector.tensor_copy(
-                    out=xgw[:, :, u], in_=words[:, u * T:(u + 1) * T].indirect(offs_t[:, e * C // 16:(e + 1) * C // 16]))
+                    out=gww[:, u * C:(u + 1) * C], in_=words[:, u * T:(u + 1) * T].indirect(offs_t[:, e * C // 16:(e + 1) * C // 16]))
+            elif k == "I":
+                e = n[0]
+                xg = get(f"xg{e}", lambda: ring.tile([P, 4 * C], BF16, name="xg", align_bytes=64))
+                copy_on("S", xg[:].rearrange("p (n u e) -> p n u e", u=2, e=2), st[f"gw{e}"][:].rearrange("p u n e -> p n u e"))
             elif k == "QX":
                 st[f"xq{n[0]}"] = quantize(st[f"xg{n[0]}"][:], C, f"xq{n[0]}")
             elif k == "XS":
-                nc.vector.tensor_copy(out=xs[:], in_=xw[:].rearrange("p u t e -> p t u e"))
+                a, b = n[1:]
+                copy_on(eng[0], xs[:].rearrange("p t u e -> p (t u e)").rearrange("p (c i j) -> p c j i", i=4, j=4)[:, a // 4:b // 4],
+                        x_raw[:].rearrange("p j (c i) -> p c j i", i=4)[:, a // 4:b // 4])
             elif k == "XQ":
                 st["xq4"] = quantize(xs[:].rearrange("p t u e -> p (t u e)"), T, "xsq")
             elif k == "W1":
@@ -245,7 +257,7 @@ def tile_moe_shr_mlp_gelu_kernel(tc, xT, w1, w2, gate, offs, pos1, pos2, out):
                 st[f"w1q{n[0]}"] = quantize(st[f"g1{n[0]}"][:], H, f"w1q{n[0]}")
             elif k == "W2":
                 e, h, a, b = n
-                g = get(f"g2{e}_{h}", lambda: group2.tile([P, 2 * N], BF16, name="wg2", align_bytes=64))
+                g = get(f"g2{e}_{h}", lambda: group2.tile([P, 2 * N], BF16, name="work", align_bytes=64) if e < E else group.tile([P, 2 * N], BF16, name="wg1", align_bytes=64))
                 copy_on(eng[0], g[:].rearrange("p (c i j) -> p c j i", i=4, j=4)[:, a // 4:b // 4],
                         w2_raw[e][h][:].rearrange("p j (c i) -> p c j i", i=4)[:, a // 4:b // 4])
             elif k == "Q2":
@@ -283,12 +295,12 @@ def tile_moe_shr_mlp_gelu_kernel(tc, xT, w1, w2, gate, offs, pos1, pos2, out):
                 st[f"ys{m}"] = bank
             elif k == "GA":
                 m = n[0]
-                first = ring.tile([P, T], F32, name="first")
+                first = group2.tile([P, T], F32, name="work", align_bytes=64)
                 st[f"ga{m}"] = first
                 nc.vector.tensor_tensor(first[:], y[m][:].indirect(pos_t[0][:]), gates[:, 0, :], MULT)
             elif k == "GB":
                 m = n[0]
-                second = ring.tile([P, T], F32, name="second")
+                second = group2.tile([P, T], F32, name="work", align_bytes=64)
                 st[f"gb{m}"] = second
                 nc.vector.tensor_tensor(second[:], y[m][:].indirect(pos_t[1][:]), gates[:, 1, :], MULT)
             elif k == "AD":

@@ -17,138 +17,142 @@ P = 128
 FLOPS = 2 * (E * C + T) * (K * H + H * N)
 BYTES = 4 * (K * T + (E + 1) * (K * H + H * N) + 2 * T + N * T) + 2 * P * (E * C + 2 * T) // 16
 
-DMA = ["x0","x1","w10","w11","w12","w13","w20.0","w21.0","w22.0","w23.0","gate","w20.1","w21.1","w22.1","w23.1","w14","w24.0","w24.1"]
+DMA = ["x0a","x0b","x1","w10","w11","w12","w13","w20.0","w21.0","w22.0","w23.0","gate","w20.1","w21.1","w22.1","w23.1","w14","w24.0","w24.1"]
 ORDER = """
-X 0 V 0 448;
-X 0 S 448 512;
+X 0 V 0 256;
+X 0 V 256 512;
 G 0 0;
-X 1 S 192 512;
-X 1 V 0 192;
+X 1 S 0 512;
+XS 0 G 0 128;
 G 1 0;
-XS 0 S 256 512;
 G 2 0;
+XS 0 G 128 256;
 G 3 0;
-W1 0 S 48 128;
+XS 0 G 256 384;
+W1 0 S 0 64;
 G 0 1;
 G 1 1;
+XS 0 G 384 512;
 G 2 1;
 I 0;
 G 3 1;
+W1 0 S 64 128;
+W1 1 V 0 128;
 I 1;
-W1 0 V 0 48;
 QX 0;
-W1 1 S 48 128;
-Q1 0;
-QX 1;
-W1 1 V 0 48;
-M 0 0;
+Q1 1;
 I 2;
+Q1 0;
+W1 2 S 64 128;
+QX 1;
+QX 2;
+M 0 0;
+W1 2 V 0 64;
 M 0 1;
-W1 2 V 0 128;
+I 3;
+W1 3 V 0 128;
 A 0 0;
 A 0 1;
-Q1 1;
-I 3;
-QX 2;
-QH 0;
 M 1 0;
-W1 3 S 96 128;
+W2 0.0 S 128 256;
 Q1 2;
 M 1 1;
+QH 0;
 A 1 0;
 QX 3;
-W1 3 V 0 96;
+Q1 3;
 A 1 1;
 M 2 0;
-W2 0.0 S 128 256;
 W2 0.0 V 0 128;
+W2 2.0 S 128 256;
+W2 1.0 V 0 256;
 M 2 1;
-QH 1;
 A 2 0;
-Q1 3;
+QH 1;
 A 2 1;
 Q2 0.0;
-W2 1.0 V 0 96;
-W2 1.0 S 96 256;
-M 3 0;
-W2 2.0 V 0 256;
-M 3 1;
-A 3 0;
 Q2 1.0;
-A 3 1;
-Q2 2.0;
-W2 3.0 V 0 224;
+M 3 0;
+W2 3.0 S 128 256;
+W2 2.0 V 0 128;
+M 3 1;
 QH 2;
+A 3 0;
 N 0 0;
-W2 3.0 S 224 256;
+Q2 2.0;
 N 0 1;
-QH 3;
+W2 3.0 V 0 128;
+A 3 1;
+XQ;
 Y 0 0;
 Q2 3.0;
-XS 0 V 0 256;
 Y 0 1;
+QH 3;
+W2 1.1 V 0 256;
+W2 0.1 S 0 256;
 N 1 0;
-W2 0.1 V 0 96;
-W2 0.1 S 96 256;
-XQ;
 N 1 1;
+Q2 1.1;
+W2 2.1 V 0 256;
 Y 1 0;
 Q2 0.1;
 Y 1 1;
-W2 1.1 V 0 192;
-W2 1.1 S 192 256;
-GA 0;
-W2 2.1 S 0 256;
-Q2 1.1;
-GB 0;
-N 0 2;
-W2 3.1 S 0 256;
-N 0 3;
 Q2 2.1;
-AD 0;
+W2 3.1 S 0 256;
+GA 0;
+N 0 2;
+N 0 3;
+GB 0;
 Y 0 2;
 GA 1;
 Y 0 3;
-W1 4 S 16 72;
+W1 4 S 0 64;
 Q2 3.1;
-W1 4 V 0 16;
-GB 1;
+AD 0;
 N 1 2;
+GB 1;
 N 1 3;
-W1 4 S 72 128;
-W2 4.0 V 0 32;
+W1 4 S 64 128;
 AD 1;
 Y 1 2;
-W2 4.1 V 0 160;
 Q1 4;
 Y 1 3;
 GA 2;
-W2 4.0 S 32 256;
+W2 4.0 S 0 256;
 M 4 0;
 M 4 1;
 GB 2;
 A 4 0;
+GA 3;
 A 4 1;
 M 4 2;
+W2 4.1 S 0 256;
 Q2 4.0;
-W2 4.1 S 160 256;
-AD 2;
 M 4 3;
+QH 4.0;
+AD 2;
+S 0.0;
+GB 3;
 A 4 2;
-GA 3;
+S 1.0;
 A 4 3;
 Q2 4.1;
-QH 4;
-GB 3;
-S 0;
-S 1;
-S 2;
-F 0;
-S 3;
 AD 3;
-F 1;
-F 2;
-F 3
+S 2.0;
+QH 4.1;
+S 3.0;
+F 0.0;
+F 1.0;
+S 0.1;
+F 2.0;
+S 1.1;
+S 2.1;
+F 3.0;
+S 3.1;
+F 0.1;
+F 1.1;
+F 2.1;
+F 3.1
 """
 
 
@@ -176,7 +180,8 @@ def tile_moe_shr_mlp_gelu_kernel(tc, xT, w1, w2, gate, offs, pos1, pos2, out):
         for d in DMA:
             if d.startswith("x"):
                 u = int(d[1])
-                nc.sync.dma_start(out=x_raw[:, 2 * u:2 * u + 2, :], in_=xr[:, 2 * u:2 * u + 2, :])
+                a, b = {"a": (0, 256), "b": (256, 512)}.get(d[2:], (0, 512))
+                nc.sync.dma_start(out=x_raw[:, 2 * u:2 * u + 2, a:b], in_=xr[:, 2 * u:2 * u + 2, a:b])
             elif d == "gate":
                 nc.sync.dma_start(pos_t[0][:], pos1)
                 nc.sync.dma_start(pos_t[1][:], pos2)
@@ -244,8 +249,11 @@ def tile_moe_shr_mlp_gelu_kernel(tc, xT, w1, w2, gate, offs, pos1, pos2, out):
                 st[f"xq{n[0]}"] = quantize(st[f"xg{n[0]}"][:], C, f"xq{n[0]}")
             elif k == "XS":
                 a, b = n[1:]
-                copy_on(eng[0], xs[:].rearrange("p t u e -> p (t u e)").rearrange("p (c i j) -> p c j i", i=4, j=4)[:, a // 4:b // 4],
-                        x_raw[:].rearrange("p j (c i) -> p c j i", i=4)[:, a // 4:b // 4])
+                if eng[0] == "G":
+                    copy_on("G", xs[:].rearrange("p t u e -> p t (u e)")[:, a:b], x_raw[:, :, a:b].rearrange("p j t -> p t j"))
+                else:
+                    copy_on(eng[0], xs[:].rearrange("p t u e -> p (t u e)").rearrange("p (c i j) -> p c j i", i=4, j=4)[:, a // 4:b // 4],
+                            x_raw[:].rearrange("p j (c i) -> p c j i", i=4)[:, a // 4:b // 4])
             elif k == "XQ":
                 st["xq4"] = quantize(xs[:].rearrange("p t u e -> p (t u e)"), T, "xsq")
             elif k == "W1":
@@ -278,6 +286,13 @@ def tile_moe_shr_mlp_gelu_kernel(tc, xT, w1, w2, gate, offs, pos1, pos2, out):
                 nc.scalar.activation(hg[:, P * c:P * c + P, :], st[f"ba{e}_{c}"][:].rearrange("p r n -> p n r"), GELU)
             elif k == "QH":
                 e = n[0]
+                if e == E:
+                    t = n[1]
+                    codes, scales = get("hq4", lambda: (keep.tile([P, T], U32, name="hsq_c", align_bytes=64), keep.tile([P, T], U8, name="hsq_s", align_bytes=64)))
+                    half = slice(256 * t, 256 * t + 256)
+                    nc.vector.quantize_mx(out=codes[:, half].bitcast(FP8X4), scales=scales[:, half],
+                                          in_=st["hg4"][:, half, :].rearrange("p n r -> p (n r)"))
+                    continue
                 st[f"hq{e}"] = quantize(st[f"hg{e}"][:].rearrange("p n r -> p (n r)"), C if e < E else T, f"hq{e}")
             elif k == "N":
                 pr, m = n
@@ -289,10 +304,15 @@ def tile_moe_shr_mlp_gelu_kernel(tc, xT, w1, w2, gate, offs, pos1, pos2, out):
                 pr, m = n
                 copy_on("S", y[m][:, 512 * pr:512 * pr + 512], st[f"by{pr}_{m}"][:].rearrange("p i n -> p (i n)"))
             elif k == "S":
-                m = n[0]
-                bank = psum_s.tile([P, T], F32, name=f"bank_s{m}")
-                mx(bank[:], st[f"w2q4_{m // 2}"], slice(P * (m % 2), P * (m % 2) + P), st["hq4"], slice(0, T))
-                st[f"ys{m}"] = bank
+                m, t = n
+                if t == 0:
+                    bank = psum_s.tile([P, T], F32, name=f"bank_s{m}")
+                elif m < 2:
+                    bank = psum_y.tile([P, T], F32, name="bank_y")
+                else:
+                    bank = psum_a.tile([P, T], F32, name="bank_a")
+                mx(bank[:, 0:256], st[f"w2q4_{m // 2}"], slice(P * (m % 2), P * (m % 2) + P), st["hq4"], slice(256 * t, 256 * t + 256))
+                st[f"ys{m}.{t}"] = bank
             elif k == "GA":
                 m = n[0]
                 first = group2.tile([P, T], F32, name="work", align_bytes=64)
@@ -309,7 +329,8 @@ def tile_moe_shr_mlp_gelu_kernel(tc, xT, w1, w2, gate, offs, pos1, pos2, out):
                 st[f"ad{m}"] = both
                 nc.vector.tensor_tensor(both[:], st[f"ga{m}"][:], st[f"gb{m}"][:], ADD)
             elif k == "F":
-                m = n[0]
-                res = ring.tile([P, T], F32, name="res")
-                nc.vector.tensor_tensor(res[:], st[f"ys{m}"][:], st[f"ad{m}"][:], ADD)
-                nc.sync.dma_start(out=out[P * m:P * m + P, :], in_=res[:])
+                m, t = n
+                half = slice(256 * t, 256 * t + 256)
+                res = keep.tile([P, 256], F32, name=f"res{m}_{t}")
+                nc.vector.tensor_tensor(res[:], st[f"ys{m}.{t}"][:, 0:256], st[f"ad{m}"][:, half], ADD)
+                nc.sync.dma_start(out=out[P * m:P * m + P, half], in_=res[:])

@@ -259,15 +259,15 @@ def tile_moe_shr_mlp_gelu_kernel(tc, xT, w1, w2, gate, offs, pos1, pos2, out):
             elif k == "W1":
                 e, a, b = n
                 g = get(f"g1{e}", lambda: group.tile([P, 4 * H], BF16, name="wg1", align_bytes=64))
-                copy_on(eng[0], g[:].rearrange("p (t m j) -> p m j t", t=4, j=4)[:, a:b],
-                        w1_raw[e][:].rearrange("p j (m t) -> p m j t", t=4)[:, a:b])
+                copy_on(eng[0], g[:].rearrange("p (t m u e) -> p m u t e", t=4, u=2, e=2)[:, a:b],
+                        w1_raw[e][:].rearrange("p (u e) (m t) -> p m u t e", u=2, t=4)[:, a:b])
             elif k == "Q1":
                 st[f"w1q{n[0]}"] = quantize(st[f"g1{n[0]}"][:], H, f"w1q{n[0]}")
             elif k == "W2":
                 e, h, a, b = n
                 g = get(f"g2{e}_{h}", lambda: group2.tile([P, 2 * N], BF16, name="work", align_bytes=64) if e < E else group.tile([P, 2 * N], BF16, name="wg1", align_bytes=64))
-                copy_on(eng[0], g[:].rearrange("p (c i j) -> p c j i", i=4, j=4)[:, a // 4:b // 4],
-                        w2_raw[e][h][:].rearrange("p j (c i) -> p c j i", i=4)[:, a // 4:b // 4])
+                copy_on(eng[0], g[:].rearrange("p (c i u e) -> p c u i e", i=4, u=2, e=2)[:, a // 4:b // 4],
+                        w2_raw[e][h][:].rearrange("p (u e) (c i) -> p c u i e", u=2, i=4)[:, a // 4:b // 4])
             elif k == "Q2":
                 e, h = n
                 st[f"w2q{e}_{h}"] = quantize(st[f"g2{e}_{h}"][:], N // 2, f"w2q{e}_{h}")

from contextlib import ExitStack

import concourse.mybir as mybir

F32 = mybir.dt.float32
BF16 = mybir.dt.bfloat16
U32 = mybir.dt.uint32
U16 = mybir.dt.uint16
U8 = mybir.dt.uint8
FP8X4 = mybir.dt.float8_e4m3fn_x4
MULT = mybir.AluOpType.mult
ADD = mybir.AluOpType.add
GELU = mybir.ActivationFunctionType.Gelu_apprx_tanh

K, T, E, C, H, N = 512, 512, 4, 256, 512, 512
P = 128
FLOPS = 2 * (E * C + T) * (K * H + H * N)
BYTES = 4 * (K * T + (E + 1) * (K * H + H * N) + 2 * T + N * T) + 2 * P * (E * C + 2 * T) // 16

DMA = ["x0a","x0b","x1","w10","w11","w12","w13","w20.0","w21.0","w22.0","w23.0","gate","w20.1","w21.1","w22.1","w23.1","w14","w24.0","w24.1"]
ORDER = """
X 0 V 0 256;
X 0 V 256 512;
G 0 0;
X 1 S 0 512;
XS 0 G 0 128;
G 1 0;
G 2 0;
XS 0 G 128 256;
G 3 0;
XS 0 G 256 384;
W1 0 S 0 64;
G 0 1;
G 1 1;
XS 0 G 384 512;
G 2 1;
I 0;
G 3 1;
W1 0 S 64 128;
W1 1 V 0 128;
I 1;
QX 0;
Q1 1;
I 2;
Q1 0;
W1 2 S 64 128;
QX 1;
QX 2;
M 0 0;
W1 2 V 0 64;
M 0 1;
I 3;
W1 3 V 0 128;
A 0 0;
A 0 1;
M 1 0;
W2 0.0 S 128 256;
Q1 2;
M 1 1;
QH 0;
A 1 0;
QX 3;
Q1 3;
A 1 1;
M 2 0;
W2 0.0 V 0 128;
W2 2.0 S 128 256;
W2 1.0 V 0 256;
M 2 1;
A 2 0;
QH 1;
A 2 1;
Q2 0.0;
Q2 1.0;
M 3 0;
W2 3.0 S 128 256;
W2 2.0 V 0 128;
M 3 1;
QH 2;
A 3 0;
N 0 0;
Q2 2.0;
N 0 1;
W2 3.0 V 0 128;
A 3 1;
XQ;
Y 0 0;
Q2 3.0;
Y 0 1;
QH 3;
W2 1.1 V 0 256;
W2 0.1 S 0 256;
N 1 0;
N 1 1;
Q2 1.1;
W2 2.1 V 0 256;
Y 1 0;
Q2 0.1;
Y 1 1;
Q2 2.1;
W2 3.1 S 0 256;
GA 0;
N 0 2;
N 0 3;
GB 0;
Y 0 2;
GA 1;
Y 0 3;
W1 4 S 0 64;
Q2 3.1;
AD 0;
N 1 2;
GB 1;
N 1 3;
W1 4 S 64 128;
AD 1;
Y 1 2;
Q1 4;
Y 1 3;
GA 2;
W2 4.0 S 0 256;
M 4 0;
M 4 1;
GB 2;
A 4 0;
GA 3;
A 4 1;
M 4 2;
W2 4.1 S 0 256;
Q2 4.0;
M 4 3;
QH 4.0;
AD 2;
S 0.0;
GB 3;
A 4 2;
S 1.0;
A 4 3;
Q2 4.1;
AD 3;
S 2.0;
QH 4.1;
S 3.0;
F 0.0;
F 1.0;
S 0.1;
F 2.0;
S 1.1;
S 2.1;
F 3.0;
S 3.1;
F 0.1;
F 1.1;
F 2.1;
F 3.1
"""


def tile_moe_shr_mlp_gelu_kernel(tc, xT, w1, w2, gate, offs, pos1, pos2, out):
    nc = tc.nc
    with ExitStack() as ctx:
        lists = ctx.enter_context(tc.tile_pool(name="lists", bufs=1))
        keep = ctx.enter_context(tc.tile_pool(name="keep", bufs=1))
        group = ctx.enter_context(tc.tile_pool(name="group", bufs=4))
        group2 = ctx.enter_context(tc.tile_pool(name="group2", bufs=4))
        ring = ctx.enter_context(tc.tile_pool(name="ring", bufs=4))
        psum_a = ctx.enter_context(tc.psum_pool(name="psum_a", bufs=2))
        psum_y = ctx.enter_context(tc.psum_pool(name="psum_y", bufs=2))
        psum_s = ctx.enter_context(tc.psum_pool(name="psum_s", bufs=1))

        offs_t = lists.tile([P, E * C // 16], U16, name="offs_t")
        pos_t = [lists.tile([P, T // 16], U16, name=f"pos_t{r}") for r in range(2)]
        x_raw = keep.tile([P, 4, T], F32, name="x_raw")
        w1_raw = [keep.tile([P, 4, H], F32, name=f"w1_raw{e}") for e in range(E + 1)]
        w2_raw = [[keep.tile([P, 4, N // 2], F32, name=f"w2_raw{e}_{h}") for h in range(2)] for e in range(E + 1)]
        gates = keep.tile([P, 2, T], F32, name="gates")

        xr = xT.rearrange("(p j) t -> p j t", j=4)
        nc.sync.dma_start(offs_t[:], offs)
        for d in DMA:
            if d.startswith("x"):
                u = int(d[1])
                a, b = {"a": (0, 256), "b": (256, 512)}.get(d[2:], (0, 512))
                nc.sync.dma_start(out=x_raw[:, 2 * u:2 * u + 2, a:b], in_=xr[:, 2 * u:2 * u + 2, a:b])
            elif d == "gate":
                nc.sync.dma_start(pos_t[0][:], pos1)
                nc.sync.dma_start(pos_t[1][:], pos2)
                nc.sync.dma_start(out=gates[:], in_=gate[:, 0:P, :].rearrange("g p t -> p g t"))
            elif d.startswith("w1"):
                e = int(d[2])
                nc.sync.dma_start(out=w1_raw[e][:], in_=w1[e].rearrange("(p j) i -> p j i", j=4))
            else:
                e, h = int(d[2]), int(d[4])
                nc.sync.dma_start(out=w2_raw[e][h][:], in_=w2[e].rearrange("(p j) n -> p j n", j=4)[:, :, h * 256:(h + 1) * 256])

        warm = keep.tile([P, 1], F32, name="warm")
        nc.vector.memset(warm[:], 0.0)
        nc.scalar.activation(warm[:], warm[:], GELU)

        def copy_on(engine, dst, src):
            if engine == "V":
                nc.vector.tensor_copy(out=dst, in_=src)
            elif engine == "S":
                nc.scalar.copy(out=dst, in_=src)
            else:
                nc.gpsimd.tensor_scalar(out=dst, in0=src, scalar1=1.0, scalar2=0.0, op0=MULT, op1=ADD)

        def quantize(grouped, width, name):
            codes = keep.tile([P, width], U32, name=name + "_c", align_bytes=64)
            scales = keep.tile([P, width], U8, name=name + "_s", align_bytes=64)
            nc.vector.quantize_mx(out=codes[:].bitcast(FP8X4), scales=scales[:], in_=grouped)
            return codes, scales

        def mx(dst, a, acols, b, bcols):
            nc.tensor.matmul_mx(
                out=dst, lhsT=a[0][:, acols].bitcast(FP8X4), lhsT_scale=a[1][:, acols],
                rhs=b[0][:, bcols].bitcast(FP8X4), rhs_scale=b[1][:, bcols], start=True, stop=True)

        xw = keep.tile([P, 2, T, 2], BF16, name="xw", align_bytes=64)
        words = xw[:].rearrange("p u t e -> p (u t e)").bitcast(U32)
        y = [keep.tile([P, E * C], F32, name=f"y{m}") for m in range(4)]
        xs = keep.tile([P, T, 2, 2], BF16, name="xs", align_bytes=64)
        st = {}

        def get(key, make):
            if key not in st:
                st[key] = make()
            return st[key]

        for step in ORDER.replace("\n", "").split(";"):
            f = step.split()
            k = f[0]
            n = [int(z) for part in f[1:] if part not in ("V", "S", "G") for z in part.split(".")]
            eng = [z for z in f[1:] if z in ("V", "S", "G")]
            if k == "X":
                u, a, b = n
                copy_on(eng[0], xw[:, u, a:b], x_raw[:, 2 * u:2 * u + 2, a:b].rearrange("p e t -> p t e"))
            elif k == "G":
                e, u = n
                gw = get(f"gw{e}", lambda: keep.tile([P, 2, C, 2], BF16, name=f"gw{e}", align_bytes=64))
                gww = gw[:].rearrange("p u n e -> p (u n e)").bitcast(U32)
                nc.vector.tensor_copy(
                    out=gww[:, u * C:(u + 1) * C], in_=words[:, u * T:(u + 1) * T].indirect(offs_t[:, e * C // 16:(e + 1) * C // 16]))
            elif k == "I":
                e = n[0]
                xg = get(f"xg{e}", lambda: ring.tile([P, 4 * C], BF16, name="xg", align_bytes=64))
                copy_on("S", xg[:].rearrange("p (n u e) -> p n u e", u=2, e=2), st[f"gw{e}"][:].rearrange("p u n e -> p n u e"))
            elif k == "QX":
                st[f"xq{n[0]}"] = quantize(st[f"xg{n[0]}"][:], C, f"xq{n[0]}")
            elif k == "XS":
                a, b = n[1:]
                if eng[0] == "G":
                    copy_on("G", xs[:].rearrange("p t u e -> p t (u e)")[:, a:b], x_raw[:, :, a:b].rearrange("p j t -> p t j"))
                else:
                    copy_on(eng[0], xs[:].rearrange("p t u e -> p (t u e)").rearrange("p (c i j) -> p c j i", i=4, j=4)[:, a // 4:b // 4],
                            x_raw[:].rearrange("p j (c i) -> p c j i", i=4)[:, a // 4:b // 4])
            elif k == "XQ":
                st["xq4"] = quantize(xs[:].rearrange("p t u e -> p (t u e)"), T, "xsq")
            elif k == "W1":
                e, a, b = n
                g = get(f"g1{e}", lambda: group.tile([P, 4 * H], BF16, name="wg1", align_bytes=64))
                copy_on(eng[0], g[:].rearrange("p (t m u e) -> p m u t e", t=4, u=2, e=2)[:, a:b],
                        w1_raw[e][:].rearrange("p (u e) (m t) -> p m u t e", u=2, t=4)[:, a:b])
            elif k == "Q1":
                st[f"w1q{n[0]}"] = quantize(st[f"g1{n[0]}"][:], H, f"w1q{n[0]}")
            elif k == "W2":
                e, h, a, b = n
                g = get(f"g2{e}_{h}", lambda: group2.tile([P, 2 * N], BF16, name="work", align_bytes=64) if e < E else group.tile([P, 2 * N], BF16, name="wg1", align_bytes=64))
                copy_on(eng[0], g[:].rearrange("p (c i u e) -> p c u i e", i=4, u=2, e=2)[:, a // 4:b // 4],
                        w2_raw[e][h][:].rearrange("p (u e) (c i) -> p c u i e", u=2, i=4)[:, a // 4:b // 4])
            elif k == "Q2":
                e, h = n
                st[f"w2q{e}_{h}"] = quantize(st[f"g2{e}_{h}"][:], N // 2, f"w2q{e}_{h}")
            elif k == "M":
                e, c = n
                bank = psum_a.tile([P, 4, P], F32, name="bank_a")
                st[f"ba{e}_{c}"] = bank
                for r in range(4):
                    mx(bank[:, r, :], st[f"w1q{e}"], slice(P * r, P * r + P), st[f"xq{e}"], slice(P * c, P * c + P))
            elif k == "A":
                e, c = n
                if e < E:
                    hg = get(f"hg{e}", lambda: ring.tile([P, C, 4], BF16, name="hg", align_bytes=64))
                else:
                    hg = get(f"hg{e}", lambda: keep.tile([P, T, 4], BF16, name="hs", align_bytes=64))
                nc.scalar.activation(hg[:, P * c:P * c + P, :], st[f"ba{e}_{c}"][:].rearrange("p r n -> p n r"), GELU)
            elif k == "QH":
                e = n[0]
                if e == E:
                    t = n[1]
                    codes, scales = get("hq4", lambda: (keep.tile([P, T], U32, name="hsq_c", align_bytes=64), keep.tile([P, T], U8, name="hsq_s", align_bytes=64)))
                    half = slice(256 * t, 256 * t + 256)
                    nc.vector.quantize_mx(out=codes[:, half].bitcast(FP8X4), scales=scales[:, half],
                                          in_=st["hg4"][:, half, :].rearrange("p n r -> p (n r)"))
                    continue
                st[f"hq{e}"] = quantize(st[f"hg{e}"][:].rearrange("p n r -> p (n r)"), C if e < E else T, f"hq{e}")
            elif k == "N":
                pr, m = n
                bank = psum_y.tile([P, 2, C], F32, name="bank_y")
                st[f"by{pr}_{m}"] = bank
                for i in range(2):
                    mx(bank[:, i, :], st[f"w2q{2 * pr + i}_{m // 2}"], slice(P * (m % 2), P * (m % 2) + P), st[f"hq{2 * pr + i}"], slice(0, C))
            elif k == "Y":
                pr, m = n
                copy_on("S", y[m][:, 512 * pr:512 * pr + 512], st[f"by{pr}_{m}"][:].rearrange("p i n -> p (i n)"))
            elif k == "S":
                m, t = n
                if t == 0:
                    bank = psum_s.tile([P, T], F32, name=f"bank_s{m}")
                elif m < 2:
                    bank = psum_y.tile([P, T], F32, name="bank_y")
                else:
                    bank = psum_a.tile([P, T], F32, name="bank_a")
                mx(bank[:, 0:256], st[f"w2q4_{m // 2}"], slice(P * (m % 2), P * (m % 2) + P), st["hq4"], slice(256 * t, 256 * t + 256))
                st[f"ys{m}.{t}"] = bank
            elif k == "GA":
                m = n[0]
                first = group2.tile([P, T], F32, name="work", align_bytes=64)
                st[f"ga{m}"] = first
                nc.vector.tensor_tensor(first[:], y[m][:].indirect(pos_t[0][:]), gates[:, 0, :], MULT)
            elif k == "GB":
                m = n[0]
                second = group2.tile([P, T], F32, name="work", align_bytes=64)
                st[f"gb{m}"] = second
                nc.vector.tensor_tensor(second[:], y[m][:].indirect(pos_t[1][:]), gates[:, 1, :], MULT)
            elif k == "AD":
                m = n[0]
                both = keep.tile([P, T], F32, name=f"both{m}")
                st[f"ad{m}"] = both
                nc.vector.tensor_tensor(both[:], st[f"ga{m}"][:], st[f"gb{m}"][:], ADD)
            elif k == "F":
                m, t = n
                half = slice(256 * t, 256 * t + 256)
                res = keep.tile([P, 256], F32, name=f"res{m}_{t}")
                nc.vector.tensor_tensor(res[:], st[f"ys{m}.{t}"][:, 0:256], st[f"ad{m}"][:, half], ADD)
                nc.sync.dma_start(out=out[P * m:P * m + P, half], in_=res[:])
